import numpy as np
import ml_dtypes


def mxq(x, axis, fmt="e4m3"):
    dtype, down = {"e4m3": (ml_dtypes.float8_e4m3fn, 7), "e5m2": (ml_dtypes.float8_e5m2, 14)}[fmt]
    v = np.moveaxis(np.asarray(x, np.float32).astype(ml_dtypes.bfloat16).astype(np.float64), axis, -1)
    blocks = v.reshape(v.shape[:-1] + (-1, 32))
    amax = np.abs(blocks).max(-1, keepdims=True)
    byte = np.maximum(np.where(amax > 0, np.frexp(amax)[1] - 1 + 127, 0) - down, 1)
    scale = np.exp2(byte - 127.0)
    codes = (blocks / scale).astype(np.float32).astype(dtype).astype(np.float64)
    return np.moveaxis((codes * scale).reshape(v.shape), -1, axis)


WIDE = False


def mx_kscale(k):
    if not WIDE:
        return np.ones(k)
    levels = np.array([24, -24, 12, -12, 0])
    if k % 512:
        return np.exp2(np.random.permutation(np.resize(levels, k // 32))).repeat(32)
    a = np.empty((k // 512, 16))
    for p in range(k // 512):
        a[p, :8] = np.random.permutation(np.resize(levels, 8))
        for g in range(8):
            far = levels[np.abs(levels - a[p, g]) >= 10]
            a[p, g + 8] = far[np.random.randint(len(far))]
    return np.exp2(a.ravel()).repeat(32)


def f64(x):
    return np.asarray(x).astype(np.float64)


def striped(idx):
    return np.tile(idx.reshape(-1, 16).T, (8, 1)).astype(np.uint16)


def unstriped(offs):
    return offs[:16].T.reshape(-1).astype(np.int64)


E2M1 = np.array([0.0, 0.5, 1.0, 1.5, 2.0, 3.0, 4.0, 6.0, -0.0, -0.5, -1.0, -1.5, -2.0, -3.0, -4.0, -6.0])


def pack_weight(w, fmt):
    k, n = w.shape
    w = f64(np.asarray(w, np.float32).astype(ml_dtypes.bfloat16)).reshape(k // 32, 32, n)
    amax = np.abs(w).max(1)
    if fmt == "e4m3":
        byte = np.frexp(amax)[1] - 1 + 127 - 7
    else:
        mant, ex = np.frexp(amax / 6.0)
        byte = np.where(mant > 0.5, ex, ex - 1) + 127
    byte = np.clip(np.where(amax > 0, byte, 1), 1, 254)
    scaled = (w * np.exp2(127.0 - byte)[:, None, :]).reshape(k, n).astype(np.float32)
    by_word = np.ascontiguousarray(scaled.reshape(k // 512, 128, 4, n).transpose(0, 1, 3, 2))
    if fmt == "e4m3":
        words = by_word.astype(ml_dtypes.float8_e4m3fn).view(np.uint8)
    else:
        c = by_word.astype(ml_dtypes.float4_e2m1fn).view(np.uint8) & 0xF
        words = (c[..., 0::2] | (c[..., 1::2] << 4)).reshape(k // 512, 128, 2 * n)
    return np.ascontiguousarray(words), np.ascontiguousarray(byte.astype(np.uint8).reshape(k // 512, 16, n))


def unpack_weight(words, scales, fmt):
    g, _, n = scales.shape
    words = np.ascontiguousarray(words).reshape(g, 128, n, -1)
    if fmt == "e4m3":
        vals = words.view(ml_dtypes.float8_e4m3fn).astype(np.float64)
    else:
        nib = np.empty((g, 128, n, 4), np.uint8)
        nib[..., 0::2] = words & 0xF
        nib[..., 1::2] = words >> 4
        vals = E2M1[nib]
    vals = vals * np.repeat(np.exp2(scales.astype(np.float64) - 127.0), 8, axis=1)[..., None]
    return vals.transpose(0, 1, 3, 2).reshape(g * 512, n)


K, L, N, T, J = 512, 512, 512, 4096, 512


def setup_inputs():
    n = np.random.standard_normal
    s = mx_kscale(K)[:, None]
    s2 = mx_kscale(L)[:, None]
    p_tab = pack_weight(n((K, T)) * s, "e4m3")
    p_w = pack_weight(n((K, N)) / np.sqrt(K) / s, "e4m3")
    p_wx = pack_weight(n((L, N)) / np.sqrt(L) / s2, "e2m1")
    return {
        "tab_words": p_tab[0],
        "tab_scales": p_tab[1],
        "w_words": p_w[0],
        "w_scales": p_w[1],
        "x": (n((L, J)) * s2).astype(np.float32),
        "wx_words": p_wx[0],
        "wx_scales": p_wx[1],
        "iw0": (np.random.uniform(0.1, 0.6, J)).astype(np.float32),
        "iw1": (np.random.uniform(0.1, 0.6, J)).astype(np.float32),
        "offs": striped(np.concatenate([np.random.permutation(T)[:J] for _ in range(2)])),
    }


def reference(tab_words, tab_scales, w_words, w_scales, x, wx_words, wx_scales, iw0, iw1, offs):
    idx = unstriped(offs).reshape(2, J)
    tab_ = unpack_weight(tab_words, tab_scales, "e4m3")[:, idx]
    w_ = unpack_weight(w_words, w_scales, "e4m3")
    a0 = w_.T @ tab_[:, 0]
    a1 = w_.T @ tab_[:, 1]
    x_ = mxq(f64(x), 0, "e4m3")
    wx_ = unpack_weight(wx_words, wx_scales, "e2m1")
    ax = wx_.T @ x_
    return np.maximum(a0 * f64(iw0)[None, :] + a1 * f64(iw1)[None, :] + ax, 0.0)

@@ -1,0 +1,148 @@
+from contextlib import ExitStack
+
+import concourse.mybir as mybir
+from concourse.masks import make_identity
+
+K, L, N, T, J = 512, 512, 512, 4096, 512
+FLOPS = 2 * (2 * K + L) * N * J
+
+F32 = mybir.dt.float32
+BF16 = mybir.dt.bfloat16
+I32 = mybir.dt.int32
+U32 = mybir.dt.uint32
+U16 = mybir.dt.uint16
+U8 = mybir.dt.uint8
+FP8X4 = mybir.dt.float8_e4m3fn_x4
+FP4X4 = mybir.dt.float4_e2m1fn_x4
+ACT = mybir.ActivationFunctionType
+ALU = mybir.AluOpType
+
+P = 128
+PACK = 4
+TILES = J // P
+HALF = J // 2
+IW_ROW = P - 2 * TILES
+
+
+def load_scale_rows(queue, plane, rows):
+    for q in range(4):
+        queue.dma_start(out=plane[32 * q : 32 * q + 4, :].bitcast(I32), in_=rows[0, 4 * q : 4 * q + 4, :].bitcast(I32))
+
+
+def tile_list_interp_relu_kernel(tc, tab_words, tab_scales, w_words, w_scales, x, wx_words, wx_scales, iw0, iw1, offs, out):
+    nc = tc.nc
+    with ExitStack() as ctx:
+        keep = ctx.enter_context(tc.tile_pool(name="keep", bufs=1))
+        prod = ctx.enter_context(tc.psum_pool(name="prod", bufs=4))
+        turn = ctx.enter_context(tc.psum_pool(name="turn", bufs=1))
+
+        offsets = keep.tile([P, 2 * J // 16], U16, name="offsets")
+        nc.sync.dma_start(offsets[:], offs)
+
+        iw_rows = keep.tile([P, P], F32, name="iw_rows")
+        nc.sync.dma_start(out=iw_rows[IW_ROW : IW_ROW + TILES, :], in_=iw0.rearrange("(a b) -> a b", b=P))
+        nc.sync.dma_start(out=iw_rows[IW_ROW + TILES : P, :], in_=iw1.rearrange("(a b) -> a b", b=P))
+
+        x_raw = keep.tile([P, PACK, J], F32, name="x_raw")
+        nc.sync.dma_start(out=x_raw[:], in_=x.rearrange("(p t) j -> p t j", t=PACK))
+        wx_codes = keep.tile([P, 2 * N], U8, name="wx_codes", align_bytes=64)
+        nc.sync.dma_start(out=wx_codes[:].bitcast(I32), in_=wx_words[0].bitcast(I32))
+        table = keep.tile([P, T], I32, name="table", align_bytes=64)
+        nc.sync.dma_start(out=table[:], in_=tab_words[0].rearrange("p t i -> p (t i)").bitcast(I32))
+        w_codes = keep.tile([P, N], I32, name="w_codes", align_bytes=64)
+        nc.sync.dma_start(out=w_codes[:], in_=w_words[0].rearrange("p n i -> p (n i)").bitcast(I32))
+
+        table_plane = keep.tile([P, T], U8, name="table_plane", align_bytes=64)
+        nc.vector.memset(table_plane[:].bitcast(I32), 0)
+        load_scale_rows(nc.scalar, table_plane, tab_scales)
+
+        wx_plane = keep.tile([P, N], U8, name="wx_plane", align_bytes=64)
+        w_plane = keep.tile([P, N], U8, name="w_plane", align_bytes=64)
+        nc.gpsimd.memset(wx_plane[:].bitcast(I32), 0)
+        load_scale_rows(nc.gpsimd, wx_plane, wx_scales)
+        nc.gpsimd.memset(w_plane[:].bitcast(I32), 0)
+        load_scale_rows(nc.gpsimd, w_plane, w_scales)
+
+        identity = keep.tile([P, P], F32, name="identity")
+        make_identity(nc, identity[:])
+
+        nc.vector.memset(iw_rows[0:IW_ROW, :], 0.0)
+        iw_turned = prod.tile([P, N], F32, name="bank", tag="bank")
+        nc.tensor.transpose(iw_turned[:, 0:P], iw_rows[:], identity[:])
+        iw_cols = keep.tile([P, 2 * TILES], F32, name="iw_cols")
+        nc.scalar.activation(iw_cols[:], iw_turned[:, IW_ROW:P], ACT.Copy)
+
+        x_codes = keep.tile([P, J], U32, name="x_codes", align_bytes=64)
+        x_plane = keep.tile([P, J], U8, name="x_plane", align_bytes=64)
+        x_bf = [keep.tile([P, HALF, PACK], BF16, name="x_bf%d" % h, align_bytes=64) for h in range(2)]
+        for h in range(2):
+            src = x_raw[:, :, h * HALF : (h + 1) * HALF].rearrange("p t (c i) -> p c t i", i=4)
+            dst = x_bf[h][:].rearrange("p (c i) t -> p c t i", i=4)
+            if h == 0:
+                nc.vector.tensor_copy(out=dst, in_=src)
+            else:
+                nc.scalar.copy(out=dst, in_=src)
+        for h in range(2):
+            cols = slice(h * HALF, (h + 1) * HALF)
+            nc.vector.quantize_mx(out=x_codes[:, cols].bitcast(FP8X4), scales=x_plane[:, cols], in_=x_bf[h][:].rearrange("p j t -> p (j t)"))
+
+        lists = [offsets[:, g * (J // 16) : (g + 1) * (J // 16)] for g in range(2)]
+        picked_plane = [keep.tile([P, J], U8, name="picked_plane%d" % g, align_bytes=64) for g in range(2)]
+        for g in range(2):
+            nc.vector.tensor_copy(picked_plane[g][:], table_plane[:].indirect(lists[g]))
+
+        sums = [turn.tile([P, TILES, P], F32, name="sum%d" % jt) for jt in range(TILES)]
+
+        def turn_into_sum(jt, part, first):
+            for nt in range(TILES):
+                nc.tensor.matmul(
+                    sums[jt][:, nt, :], part[:, nt * P : (nt + 1) * P], identity[:], is_transpose=True,
+                    start=(first and nt == 0), stop=(not first and nt == TILES - 1),
+                )
+
+        skip = [keep.tile([P, N], F32, name="skip%d" % jt) for jt in range(TILES)]
+        for jt in range(TILES):
+            cols = slice(jt * P, (jt + 1) * P)
+            bank = prod.tile([P, N], F32, name="bank", tag="bank")
+            nc.tensor.matmul_mx(
+                out=bank[:], lhsT=x_codes[:, cols].bitcast(FP8X4), lhsT_scale=x_plane[:, cols],
+                rhs=wx_codes[:].bitcast(FP4X4), rhs_scale=wx_plane[:], start=True, stop=True,
+            )
+            nc.scalar.copy(out=skip[jt][:], in_=bank[:])
+        for jt in range(TILES):
+            turn_into_sum(jt, skip[jt], True)
+
+        picked = [keep.tile([P, J], U32, name="picked%d" % g, align_bytes=64) for g in range(2)]
+        for g in range(2):
+            nc.vector.tensor_copy(picked[g][:], table[:].bitcast(U32).indirect(lists[g]))
+
+        def project(g, jt):
+            cols = slice(jt * P, (jt + 1) * P)
+            bank = prod.tile([P, N], F32, name="bank", tag="bank")
+            nc.tensor.matmul_mx(
+                out=bank[:], lhsT=picked[g][:, cols].bitcast(FP8X4), lhsT_scale=picked_plane[g][:, cols],
+                rhs=w_codes[:].bitcast(FP8X4), rhs_scale=w_plane[:], start=True, stop=True,
+            )
+            return bank
+
+        first = [keep.tile([P, N], F32, name="first%d" % jt) for jt in range(TILES)]
+        for jt in range(TILES):
+            bank = project(0, jt)
+            nc.scalar.activation(first[jt][:], bank[:], ACT.Copy, scale=iw_cols[:, jt : jt + 1])
+
+        out_view = out.rearrange("(nt p) j -> p nt j", p=P)
+        both = [keep.tile([P, N], F32, name="both%d" % jt) for jt in range(TILES)]
+        result = [keep.tile([P, TILES, P], F32, name="result%d" % jt) for jt in range(TILES)]
+        for jt in range(TILES):
+            bank = project(1, jt)
+            nc.vector.scalar_tensor_tensor(
+                out=both[jt][:], in0=bank[:], scalar=iw_cols[:, TILES + jt : TILES + jt + 1], in1=first[jt][:],
+                op0=ALU.mult, op1=ALU.add,
+            )
+        for jt in range(TILES):
+            turn_into_sum(jt, both[jt], False)
+            if jt < TILES - 1:
+                nc.scalar.activation(result[jt][:], sums[jt][:], ACT.Relu)
+            else:
+                nc.vector.tensor_scalar_max(result[jt][:], sums[jt][:], 0.0)
+            nc.sync.dma_start(out=out_view[:, :, jt * P : (jt + 1) * P], in_=result[jt][:])

@@ -1,7 +1,6 @@
 from contextlib import ExitStack
 
 import concourse.mybir as mybir
-from concourse.masks import make_identity
 
 K, L, N, T, J = 512, 512, 512, 4096, 512
 FLOPS = 2 * (2 * K + L) * N * J
@@ -22,81 +21,87 @@ PACK = 4
 TILES = J // P
 HALF = J // 2
 IW_ROW = P - 2 * TILES
-
-
-def load_scale_rows(queue, plane, rows):
-    for q in range(4):
-        queue.dma_start(out=plane[32 * q : 32 * q + 4, :].bitcast(I32), in_=rows[0, 4 * q : 4 * q + 4, :].bitcast(I32))
+W_COL = 2 * J
+PLANE = W_COL + N
+ROW0 = P - 16
+EARLY = 2
 
 
 def tile_list_interp_relu_kernel(tc, tab_words, tab_scales, w_words, w_scales, x, wx_words, wx_scales, iw0, iw1, offs, out):
     nc = tc.nc
     with ExitStack() as ctx:
         keep = ctx.enter_context(tc.tile_pool(name="keep", bufs=1))
-        prod = ctx.enter_context(tc.psum_pool(name="prod", bufs=4))
+        prod = ctx.enter_context(tc.psum_pool(name="prod", bufs=6))
         turn = ctx.enter_context(tc.psum_pool(name="turn", bufs=1))
 
         offsets = keep.tile([P, 2 * J // 16], U16, name="offsets")
         nc.sync.dma_start(offsets[:], offs)
 
+        table_rows = keep.tile([P, T], U8, name="table_rows", align_bytes=64)
+        nc.sync.dma_start(out=table_rows[ROW0:P, :].bitcast(I32), in_=tab_scales[0].bitcast(I32))
+        x_raw = keep.tile([P, PACK, J], F32, name="x_raw")
+        nc.sync.dma_start(out=x_raw[:], in_=x.rearrange("(p t) j -> p t j", t=PACK))
+        wx_plane = keep.tile([P, N], U8, name="wx_plane", align_bytes=64)
+        nc.vector.memset(wx_plane[:].bitcast(I32), 0)
+        for q in range(4):
+            nc.sync.dma_start(out=wx_plane[32 * q : 32 * q + 4, :].bitcast(I32), in_=wx_scales[0, 4 * q : 4 * q + 4, :].bitcast(I32))
+        wx_codes = keep.tile([P, 2 * N], U8, name="wx_codes", align_bytes=64)
+        nc.sync.dma_start(out=wx_codes[:].bitcast(I32), in_=wx_words[0].bitcast(I32))
+        staged = keep.tile([P, PLANE], U8, name="staged", align_bytes=64)
+        nc.sync.dma_start(out=staged[ROW0:P, W_COL : W_COL + N].bitcast(I32), in_=w_scales[0].bitcast(I32))
+        table = keep.tile([P, T], I32, name="table", align_bytes=64)
+        nc.sync.dma_start(out=table[:], in_=tab_words[0].rearrange("p t i -> p (t i)").bitcast(I32))
         iw_rows = keep.tile([P, P], F32, name="iw_rows")
         nc.sync.dma_start(out=iw_rows[IW_ROW : IW_ROW + TILES, :], in_=iw0.rearrange("(a b) -> a b", b=P))
         nc.sync.dma_start(out=iw_rows[IW_ROW + TILES : P, :], in_=iw1.rearrange("(a b) -> a b", b=P))
-
-        x_raw = keep.tile([P, PACK, J], F32, name="x_raw")
-        nc.sync.dma_start(out=x_raw[:], in_=x.rearrange("(p t) j -> p t j", t=PACK))
-        wx_codes = keep.tile([P, 2 * N], U8, name="wx_codes", align_bytes=64)
-        nc.sync.dma_start(out=wx_codes[:].bitcast(I32), in_=wx_words[0].bitcast(I32))
-        table = keep.tile([P, T], I32, name="table", align_bytes=64)
-        nc.sync.dma_start(out=table[:], in_=tab_words[0].rearrange("p t i -> p (t i)").bitcast(I32))
         w_codes = keep.tile([P, N], I32, name="w_codes", align_bytes=64)
         nc.sync.dma_start(out=w_codes[:], in_=w_words[0].rearrange("p n i -> p (n i)").bitcast(I32))
 
-        table_plane = keep.tile([P, T], U8, name="table_plane", align_bytes=64)
-        nc.vector.memset(table_plane[:].bitcast(I32), 0)
-        load_scale_rows(nc.scalar, table_plane, tab_scales)
-
-        wx_plane = keep.tile([P, N], U8, name="wx_plane", align_bytes=64)
-        w_plane = keep.tile([P, N], U8, name="w_plane", align_bytes=64)
-        nc.gpsimd.memset(wx_plane[:].bitcast(I32), 0)
-        load_scale_rows(nc.gpsimd, wx_plane, wx_scales)
-        nc.gpsimd.memset(w_plane[:].bitcast(I32), 0)
-        load_scale_rows(nc.gpsimd, w_plane, w_scales)
+        nc.vector.memset(table_rows[0:ROW0, :].bitcast(I32), 0)
+        planes = keep.tile([P, PLANE], U8, name="planes", align_bytes=64)
+        nc.gpsimd.memset(planes[:].bitcast(I32), 0)
+        nc.gpsimd.memset(iw_rows[0:IW_ROW, :], 0.0)
 
         identity = keep.tile([P, P], F32, name="identity")
-        make_identity(nc, identity[:])
+        ones = keep.tile([P, 32], F32, name="ones")
+        ramp = keep.tile([P, 32], F32, name="ramp", align_bytes=64)
+        row_id = keep.tile([P, 32], F32, name="row_id", align_bytes=64)
+        nc.gpsimd.memset(ones[:], 1.0)
+        nc.gpsimd.memset(identity[:], 0.0)
+        nc.vector.tensor_tensor_scan(ramp[:], ones[:], ones[:], 0.0, ALU.mult, ALU.add)
+        nc.vector.transpose(row_id[:], ramp[:])
+        for q in range(4):
+            rows = slice(32 * q, 32 * q + 32)
+            nc.vector.tensor_tensor(identity[rows, rows], ramp[rows, :], row_id[rows, :], ALU.is_equal)
 
-        nc.vector.memset(iw_rows[0:IW_ROW, :], 0.0)
-        iw_turned = prod.tile([P, N], F32, name="bank", tag="bank")
-        nc.tensor.transpose(iw_turned[:, 0:P], iw_rows[:], identity[:])
-        iw_cols = keep.tile([P, 2 * TILES], F32, name="iw_cols")
-        nc.scalar.activation(iw_cols[:], iw_turned[:, IW_ROW:P], ACT.Copy)
+        picked_rows = keep.tile([P, 2 * J], U8, name="picked_rows", align_bytes=64)
+        nc.vector.tensor_copy(picked_rows[:], table_rows[:].indirect(offsets[:]))
+        nc.vector.tensor_copy(staged[:, 0 : 2 * J].bitcast(I32), picked_rows[:].bitcast(I32))
+        for q in range(4):
+            nc.sync.dma_start(out=planes[32 * q : 32 * q + 4, :].bitcast(I32), in_=staged[ROW0 + 4 * q : ROW0 + 4 * q + 4, :].bitcast(I32))
+        w_plane = planes[:, W_COL : W_COL + N]
+        picked_plane = [planes[:, g * J : (g + 1) * J] for g in range(2)]
+
 
         x_codes = keep.tile([P, J], U32, name="x_codes", align_bytes=64)
         x_plane = keep.tile([P, J], U8, name="x_plane", align_bytes=64)
-        x_bf = [keep.tile([P, HALF, PACK], BF16, name="x_bf%d" % h, align_bytes=64) for h in range(2)]
-        for h in range(2):
-            src = x_raw[:, :, h * HALF : (h + 1) * HALF].rearrange("p t (c i) -> p c t i", i=4)
-            dst = x_bf[h][:].rearrange("p (c i) t -> p c t i", i=4)
-            if h == 0:
-                nc.vector.tensor_copy(out=dst, in_=src)
-            else:
-                nc.scalar.copy(out=dst, in_=src)
-        for h in range(2):
-            cols = slice(h * HALF, (h + 1) * HALF)
-            nc.vector.quantize_mx(out=x_codes[:, cols].bitcast(FP8X4), scales=x_plane[:, cols], in_=x_bf[h][:].rearrange("p j t -> p (j t)"))
+        x_bf = [keep.tile([P, P, PACK], BF16, name="x_bf%d" % jt, align_bytes=64) for jt in range(TILES)]
+        for jt in range(TILES):
+            src = x_raw[:, :, jt * P : (jt + 1) * P].rearrange("p t (c i) -> p c t i", i=4)
+            dst = x_bf[jt][:].rearrange("p (c i) t -> p c t i", i=4)
+            nc.scalar.copy(out=dst, in_=src)
+        for jt in range(TILES):
+            cols = slice(jt * P, (jt + 1) * P)
+            nc.vector.quantize_mx(out=x_codes[:, cols].bitcast(FP8X4), scales=x_plane[:, cols], in_=x_bf[jt][:].rearrange("p j t -> p (j t)"))
 
         lists = [offsets[:, g * (J // 16) : (g + 1) * (J // 16)] for g in range(2)]
-        picked_plane = [keep.tile([P, J], U8, name="picked_plane%d" % g, align_bytes=64) for g in range(2)]
-        for g in range(2):
-            nc.vector.tensor_copy(picked_plane[g][:], table_plane[:].indirect(lists[g]))
 
-        sums = [turn.tile([P, TILES, P], F32, name="sum%d" % jt) for jt in range(TILES)]
+        sums = [turn.tile([P, N], F32, name="sum%d" % jt) for jt in range(EARLY)]
 
         def turn_into_sum(jt, part, first):
             for nt in range(TILES):
                 nc.tensor.matmul(
-                    sums[jt][:, nt, :], part[:, nt * P : (nt + 1) * P], identity[:], is_transpose=True,
+                    sums[jt][:, nt * P : (nt + 1) * P], part[:, nt * P : (nt + 1) * P], identity[:], is_transpose=True,
                     start=(first and nt == 0), stop=(not first and nt == TILES - 1),
                 )
 
@@ -108,9 +113,17 @@ def tile_list_interp_relu_kernel(tc, tab_words, tab_scales, w_words, w_scales, x
                 out=bank[:], lhsT=x_codes[:, cols].bitcast(FP8X4), lhsT_scale=x_plane[:, cols],
                 rhs=wx_codes[:].bitcast(FP4X4), rhs_scale=wx_plane[:], start=True, stop=True,
             )
-            nc.scalar.copy(out=skip[jt][:], in_=bank[:])
-        for jt in range(TILES):
+            if jt < 2:
+                nc.vector.tensor_copy(out=skip[jt][:], in_=bank[:])
+            else:
+                nc.scalar.copy(out=skip[jt][:], in_=bank[:])
+        for jt in range(EARLY):
             turn_into_sum(jt, skip[jt], True)
+
+        iw_turned = prod.tile([P, N], F32, name="bank", tag="bank")
+        nc.tensor.transpose(iw_turned[:, 0:P], iw_rows[:], identity[:])
+        iw_cols = keep.tile([P, 2 * TILES], F32, name="iw_cols")
+        nc.scalar.activation(iw_cols[:], iw_turned[:, IW_ROW:P], ACT.Copy)
 
         picked = [keep.tile([P, J], U32, name="picked%d" % g, align_bytes=64) for g in range(2)]
         for g in range(2):
@@ -121,7 +134,7 @@ def tile_list_interp_relu_kernel(tc, tab_words, tab_scales, w_words, w_scales, x
             bank = prod.tile([P, N], F32, name="bank", tag="bank")
             nc.tensor.matmul_mx(
                 out=bank[:], lhsT=picked[g][:, cols].bitcast(FP8X4), lhsT_scale=picked_plane[g][:, cols],
-                rhs=w_codes[:].bitcast(FP8X4), rhs_scale=w_plane[:], start=True, stop=True,
+                rhs=w_codes[:].bitcast(FP8X4), rhs_scale=w_plane, start=True, stop=True,
             )
             return bank
 
@@ -132,17 +145,27 @@ def tile_list_interp_relu_kernel(tc, tab_words, tab_scales, w_words, w_scales, x
 
         out_view = out.rearrange("(nt p) j -> p nt j", p=P)
         both = [keep.tile([P, N], F32, name="both%d" % jt) for jt in range(TILES)]
-        result = [keep.tile([P, TILES, P], F32, name="result%d" % jt) for jt in range(TILES)]
-        for jt in range(TILES):
+        result = [keep.tile([P, N], F32, name="result%d" % jt) for jt in range(TILES)]
+
+        def combine(jt):
             bank = project(1, jt)
             nc.vector.scalar_tensor_tensor(
                 out=both[jt][:], in0=bank[:], scalar=iw_cols[:, TILES + jt : TILES + jt + 1], in1=first[jt][:],
                 op0=ALU.mult, op1=ALU.add,
             )
-        for jt in range(TILES):
+
+        def finish(jt):
             turn_into_sum(jt, both[jt], False)
-            if jt < TILES - 1:
-                nc.scalar.activation(result[jt][:], sums[jt][:], ACT.Relu)
-            else:
+            if jt == 2:
                 nc.vector.tensor_scalar_max(result[jt][:], sums[jt][:], 0.0)
-            nc.sync.dma_start(out=out_view[:, :, jt * P : (jt + 1) * P], in_=result[jt][:])
+            else:
+                nc.scalar.activation(result[jt][:], sums[jt][:], ACT.Relu)
+            nc.sync.dma_start(out=out_view[:, :, jt * P : (jt + 1) * P], in_=result[jt][:].rearrange("p (nt j) -> p nt j", j=P))
+
+        for jt in range(TILES):
+            combine(jt)
+        for jt in range(TILES):
+            if jt >= EARLY:
+                sums.append(prod.tile([P, N], F32, name="bank", tag="bank"))
+                turn_into_sum(jt, skip[jt], True)
+            finish(jt)

@@ -25,6 +25,7 @@ W_COL = 2 * J
 PLANE = W_COL + N
 ROW0 = P - 16
 EARLY = 2
+T_FIRST = 1792
 
 
 def tile_list_interp_relu_kernel(tc, tab_words, tab_scales, w_words, w_scales, x, wx_words, wx_scales, iw0, iw1, offs, out):
@@ -45,12 +46,14 @@ def tile_list_interp_relu_kernel(tc, tab_words, tab_scales, w_words, w_scales, x
         nc.vector.memset(wx_plane[:].bitcast(I32), 0)
         for q in range(4):
             nc.sync.dma_start(out=wx_plane[32 * q : 32 * q + 4, :].bitcast(I32), in_=wx_scales[0, 4 * q : 4 * q + 4, :].bitcast(I32))
+        table = keep.tile([P, T], I32, name="table", align_bytes=64)
+        table_hbm = tab_words[0].rearrange("p t i -> p (t i)").bitcast(I32)
+        nc.sync.dma_start(out=table[:, 0:T_FIRST], in_=table_hbm[:, 0:T_FIRST])
         wx_codes = keep.tile([P, 2 * N], U8, name="wx_codes", align_bytes=64)
         nc.sync.dma_start(out=wx_codes[:].bitcast(I32), in_=wx_words[0].bitcast(I32))
         staged = keep.tile([P, PLANE], U8, name="staged", align_bytes=64)
         nc.sync.dma_start(out=staged[ROW0:P, W_COL : W_COL + N].bitcast(I32), in_=w_scales[0].bitcast(I32))
-        table = keep.tile([P, T], I32, name="table", align_bytes=64)
-        nc.sync.dma_start(out=table[:], in_=tab_words[0].rearrange("p t i -> p (t i)").bitcast(I32))
+        nc.sync.dma_start(out=table[:, T_FIRST:T], in_=table_hbm[:, T_FIRST:T])
         iw_rows = keep.tile([P, P], F32, name="iw_rows")
         nc.sync.dma_start(out=iw_rows[IW_ROW : IW_ROW + TILES, :], in_=iw0.rearrange("(a b) -> a b", b=P))
         nc.sync.dma_start(out=iw_rows[IW_ROW + TILES : P, :], in_=iw1.rearrange("(a b) -> a b", b=P))
@@ -96,15 +99,16 @@ def tile_list_interp_relu_kernel(tc, tab_words, tab_scales, w_words, w_scales, x
 
         lists = [offsets[:, g * (J // 16) : (g + 1) * (J // 16)] for g in range(2)]
 
-        sums = [turn.tile([P, N], F32, name="sum%d" % jt) for jt in range(EARLY)]
-
-        def turn_into_sum(jt, part, first):
-            for nt in range(TILES):
+        def turn_into(bank, part, blocks, opens):
+            for nt in blocks:
+                at = (nt - blocks[0]) * P
                 nc.tensor.matmul(
-                    sums[jt][:, nt * P : (nt + 1) * P], part[:, nt * P : (nt + 1) * P], identity[:], is_transpose=True,
-                    start=(first and nt == 0), stop=(not first and nt == TILES - 1),
+                    bank[:, at : at + P], part[:, nt * P : (nt + 1) * P], identity[:], is_transpose=True,
+                    start=(opens and nt == blocks[0]), stop=(not opens and nt == blocks[-1]),
                 )
 
+        all_blocks = list(range(TILES))
+        sums = [turn.tile([P, N], F32, name="sum%d" % jt) for jt in range(EARLY)]
         skip = [keep.tile([P, N], F32, name="skip%d" % jt) for jt in range(TILES)]
         for jt in range(TILES):
             cols = slice(jt * P, (jt + 1) * P)
@@ -118,7 +122,7 @@ def tile_list_interp_relu_kernel(tc, tab_words, tab_scales, w_words, w_scales, x
             else:
                 nc.scalar.copy(out=skip[jt][:], in_=bank[:])
         for jt in range(EARLY):
-            turn_into_sum(jt, skip[jt], True)
+            turn_into(sums[jt], skip[jt], all_blocks, True)
 
         iw_turned = prod.tile([P, N], F32, name="bank", tag="bank")
         nc.tensor.transpose(iw_turned[:, 0:P], iw_rows[:], identity[:])
@@ -147,25 +151,34 @@ def tile_list_interp_relu_kernel(tc, tab_words, tab_scales, w_words, w_scales, x
         both = [keep.tile([P, N], F32, name="both%d" % jt) for jt in range(TILES)]
         result = [keep.tile([P, N], F32, name="result%d" % jt) for jt in range(TILES)]
 
-        def combine(jt):
+        last = TILES - 1
+        halves = [all_blocks[:2], all_blocks[2:]]
+        for jt in range(TILES):
             bank = project(1, jt)
-            nc.vector.scalar_tensor_tensor(
-                out=both[jt][:], in0=bank[:], scalar=iw_cols[:, TILES + jt : TILES + jt + 1], in1=first[jt][:],
-                op0=ALU.mult, op1=ALU.add,
-            )
+            for blocks in ([all_blocks] if jt < last else halves):
+                cols = slice(blocks[0] * P, (blocks[-1] + 1) * P)
+                nc.vector.scalar_tensor_tensor(
+                    out=both[jt][:, cols], in0=bank[:, cols], scalar=iw_cols[:, TILES + jt : TILES + jt + 1],
+                    in1=first[jt][:, cols], op0=ALU.mult, op1=ALU.add,
+                )
 
-        def finish(jt):
-            turn_into_sum(jt, both[jt], False)
-            if jt == 2:
-                nc.vector.tensor_scalar_max(result[jt][:], sums[jt][:], 0.0)
+        for jt in range(TILES):
+            pieces = [all_blocks] if jt < last else halves
+            if jt < EARLY:
+                banks = [sums[jt]]
             else:
-                nc.scalar.activation(result[jt][:], sums[jt][:], ACT.Relu)
-            nc.sync.dma_start(out=out_view[:, :, jt * P : (jt + 1) * P], in_=result[jt][:].rearrange("p (nt j) -> p nt j", j=P))
-
-        for jt in range(TILES):
-            combine(jt)
-        for jt in range(TILES):
-            if jt >= EARLY:
-                sums.append(prod.tile([P, N], F32, name="bank", tag="bank"))
-                turn_into_sum(jt, skip[jt], True)
-            finish(jt)
+                banks = [prod.tile([P, N], F32, name="bank", tag="bank") for blocks in pieces]
+                for bank, blocks in zip(banks, pieces):
+                    turn_into(bank, skip[jt], blocks, True)
+            for bank, blocks in zip(banks, pieces):
+                cols = slice(blocks[0] * P, (blocks[-1] + 1) * P)
+                width = len(blocks) * P
+                turn_into(bank, both[jt], blocks, False)
+                if jt < last:
+                    nc.scalar.activation(result[jt][:, cols], bank[:, 0:width], ACT.Relu)
+                else:
+                    nc.vector.tensor_scalar_max(result[jt][:, cols], bank[:, 0:width], 0.0)
+                nc.sync.dma_start(
+                    out=out_view[:, blocks[0] : blocks[-1] + 1, jt * P : (jt + 1) * P],
+                    in_=result[jt][:, cols].rearrange("p (nt j) -> p nt j", j=P),
+                )

@@ -25,14 +25,14 @@ W_COL = 2 * J
 PLANE = W_COL + N
 ROW0 = P - 16
 EARLY = 2
-T_FIRST = 1792
 
 
 def tile_list_interp_relu_kernel(tc, tab_words, tab_scales, w_words, w_scales, x, wx_words, wx_scales, iw0, iw1, offs, out):
     nc = tc.nc
     with ExitStack() as ctx:
         keep = ctx.enter_context(tc.tile_pool(name="keep", bufs=1))
-        prod = ctx.enter_context(tc.psum_pool(name="prod", bufs=6))
+        prod = ctx.enter_context(tc.psum_pool(name="prod", bufs=4))
+        pair = ctx.enter_context(tc.psum_pool(name="pair", bufs=2))
         turn = ctx.enter_context(tc.psum_pool(name="turn", bufs=1))
 
         offsets = keep.tile([P, 2 * J // 16], U16, name="offsets")
@@ -46,14 +46,12 @@ def tile_list_interp_relu_kernel(tc, tab_words, tab_scales, w_words, w_scales, x
         nc.vector.memset(wx_plane[:].bitcast(I32), 0)
         for q in range(4):
             nc.sync.dma_start(out=wx_plane[32 * q : 32 * q + 4, :].bitcast(I32), in_=wx_scales[0, 4 * q : 4 * q + 4, :].bitcast(I32))
-        table = keep.tile([P, T], I32, name="table", align_bytes=64)
-        table_hbm = tab_words[0].rearrange("p t i -> p (t i)").bitcast(I32)
-        nc.sync.dma_start(out=table[:, 0:T_FIRST], in_=table_hbm[:, 0:T_FIRST])
         wx_codes = keep.tile([P, 2 * N], U8, name="wx_codes", align_bytes=64)
         nc.sync.dma_start(out=wx_codes[:].bitcast(I32), in_=wx_words[0].bitcast(I32))
         staged = keep.tile([P, PLANE], U8, name="staged", align_bytes=64)
         nc.sync.dma_start(out=staged[ROW0:P, W_COL : W_COL + N].bitcast(I32), in_=w_scales[0].bitcast(I32))
-        nc.sync.dma_start(out=table[:, T_FIRST:T], in_=table_hbm[:, T_FIRST:T])
+        table = keep.tile([P, T], I32, name="table", align_bytes=64)
+        nc.sync.dma_start(out=table[:], in_=tab_words[0].rearrange("p t i -> p (t i)").bitcast(I32))
         iw_rows = keep.tile([P, P], F32, name="iw_rows")
         nc.sync.dma_start(out=iw_rows[IW_ROW : IW_ROW + TILES, :], in_=iw0.rearrange("(a b) -> a b", b=P))
         nc.sync.dma_start(out=iw_rows[IW_ROW + TILES : P, :], in_=iw1.rearrange("(a b) -> a b", b=P))
@@ -81,7 +79,7 @@ def tile_list_interp_relu_kernel(tc, tab_words, tab_scales, w_words, w_scales, x
         nc.vector.tensor_copy(picked_rows[:], table_rows[:].indirect(offsets[:]))
         nc.vector.tensor_copy(staged[:, 0 : 2 * J].bitcast(I32), picked_rows[:].bitcast(I32))
         for q in range(4):
-            nc.sync.dma_start(out=planes[32 * q : 32 * q + 4, :].bitcast(I32), in_=staged[ROW0 + 4 * q : ROW0 + 4 * q + 4, :].bitcast(I32))
+            nc.scalar.dma_start(out=planes[32 * q : 32 * q + 4, :].bitcast(I32), in_=staged[ROW0 + 4 * q : ROW0 + 4 * q + 4, :].bitcast(I32))
         w_plane = planes[:, W_COL : W_COL + N]
         picked_plane = [planes[:, g * J : (g + 1) * J] for g in range(2)]
 
@@ -99,30 +97,37 @@ def tile_list_interp_relu_kernel(tc, tab_words, tab_scales, w_words, w_scales, x
 
         lists = [offsets[:, g * (J // 16) : (g + 1) * (J // 16)] for g in range(2)]
 
-        def turn_into(bank, part, blocks, opens):
+        def turn_into(bank, part, blocks, opens, closes):
             for nt in blocks:
                 at = (nt - blocks[0]) * P
                 nc.tensor.matmul(
                     bank[:, at : at + P], part[:, nt * P : (nt + 1) * P], identity[:], is_transpose=True,
-                    start=(opens and nt == blocks[0]), stop=(not opens and nt == blocks[-1]),
+                    start=(opens and nt == blocks[0]), stop=(closes and nt == blocks[-1]),
                 )
 
+        last = TILES - 1
         all_blocks = list(range(TILES))
         sums = [turn.tile([P, N], F32, name="sum%d" % jt) for jt in range(EARLY)]
         skip = [keep.tile([P, N], F32, name="skip%d" % jt) for jt in range(TILES)]
-        for jt in range(TILES):
+
+        def project_skip(jt):
             cols = slice(jt * P, (jt + 1) * P)
-            bank = prod.tile([P, N], F32, name="bank", tag="bank")
+            bank = pair.tile([P, N], F32, name="pair_bank", tag="pair_bank")
             nc.tensor.matmul_mx(
                 out=bank[:], lhsT=x_codes[:, cols].bitcast(FP8X4), lhsT_scale=x_plane[:, cols],
                 rhs=wx_codes[:].bitcast(FP4X4), rhs_scale=wx_plane[:], start=True, stop=True,
             )
-            if jt < 2:
+            if jt < EARLY:
                 nc.vector.tensor_copy(out=skip[jt][:], in_=bank[:])
             else:
                 nc.scalar.copy(out=skip[jt][:], in_=bank[:])
+
         for jt in range(EARLY):
-            turn_into(sums[jt], skip[jt], all_blocks, True)
+            project_skip(jt)
+        for jt in range(EARLY):
+            turn_into(sums[jt], skip[jt], all_blocks, True, False)
+        for jt in range(EARLY, TILES):
+            project_skip(jt)
 
         iw_turned = prod.tile([P, N], F32, name="bank", tag="bank")
         nc.tensor.transpose(iw_turned[:, 0:P], iw_rows[:], identity[:])
@@ -135,7 +140,10 @@ def tile_list_interp_relu_kernel(tc, tab_words, tab_scales, w_words, w_scales, x
 
         def project(g, jt):
             cols = slice(jt * P, (jt + 1) * P)
-            bank = prod.tile([P, N], F32, name="bank", tag="bank")
+            if g == 1 and jt < 2:
+                bank = pair.tile([P, N], F32, name="pair_bank", tag="pair_bank")
+            else:
+                bank = prod.tile([P, N], F32, name="bank", tag="bank")
             nc.tensor.matmul_mx(
                 out=bank[:], lhsT=picked[g][:, cols].bitcast(FP8X4), lhsT_scale=picked_plane[g][:, cols],
                 rhs=w_codes[:].bitcast(FP8X4), rhs_scale=w_plane, start=True, stop=True,
@@ -143,15 +151,20 @@ def tile_list_interp_relu_kernel(tc, tab_words, tab_scales, w_words, w_scales, x
             return bank
 
         first = [keep.tile([P, N], F32, name="first%d" % jt) for jt in range(TILES)]
-        for jt in range(TILES):
+        for jt in [0, last] + list(range(1, last)):
             bank = project(0, jt)
-            nc.scalar.activation(first[jt][:], bank[:], ACT.Copy, scale=iw_cols[:, jt : jt + 1])
+            if jt < last:
+                nc.scalar.activation(first[jt][:], bank[:], ACT.Copy, scale=iw_cols[:, jt : jt + 1])
+            else:
+                nc.vector.scalar_tensor_tensor(
+                    out=first[jt][:], in0=bank[:], scalar=iw_cols[:, jt : jt + 1], in1=skip[jt][:],
+                    op0=ALU.mult, op1=ALU.add,
+                )
 
         out_view = out.rearrange("(nt p) j -> p nt j", p=P)
         both = [keep.tile([P, N], F32, name="both%d" % jt) for jt in range(TILES)]
         result = [keep.tile([P, N], F32, name="result%d" % jt) for jt in range(TILES)]
 
-        last = TILES - 1
         halves = [all_blocks[:2], all_blocks[2:]]
         for jt in range(TILES):
             bank = project(1, jt)
@@ -164,16 +177,18 @@ def tile_list_interp_relu_kernel(tc, tab_words, tab_scales, w_words, w_scales, x
 
         for jt in range(TILES):
             pieces = [all_blocks] if jt < last else halves
-            if jt < EARLY:
-                banks = [sums[jt]]
-            else:
-                banks = [prod.tile([P, N], F32, name="bank", tag="bank") for blocks in pieces]
-                for bank, blocks in zip(banks, pieces):
-                    turn_into(bank, skip[jt], blocks, True)
-            for bank, blocks in zip(banks, pieces):
+            for blocks in pieces:
+                if jt < EARLY:
+                    bank = sums[jt]
+                elif blocks[0] == 0:
+                    bank = prod.tile([P, N], F32, name="bank", tag="bank")
+                else:
+                    bank = pair.tile([P, N], F32, name="pair_bank", tag="pair_bank")
+                if EARLY <= jt < last:
+                    turn_into(bank, skip[jt], blocks, True, False)
                 cols = slice(blocks[0] * P, (blocks[-1] + 1) * P)
                 width = len(blocks) * P
-                turn_into(bank, both[jt], blocks, False)
+                turn_into(bank, both[jt], blocks, jt == last, True)
                 if jt < last:
                     nc.scalar.activation(result[jt][:, cols], bank[:, 0:width], ACT.Relu)
                 else:

from contextlib import ExitStack

import concourse.mybir as mybir

K, L, N, T, J = 512, 512, 512, 4096, 512
FLOPS = 2 * (2 * K + L) * N * J

F32 = mybir.dt.float32
BF16 = mybir.dt.bfloat16
I32 = mybir.dt.int32
U32 = mybir.dt.uint32
U16 = mybir.dt.uint16
U8 = mybir.dt.uint8
FP8X4 = mybir.dt.float8_e4m3fn_x4
FP4X4 = mybir.dt.float4_e2m1fn_x4
ACT = mybir.ActivationFunctionType
ALU = mybir.AluOpType

P = 128
PACK = 4
TILES = J // P
HALF = J // 2
IW_ROW = P - 2 * TILES
W_COL = 2 * J
PLANE = W_COL + N
ROW0 = P - 16
EARLY = 2


def tile_list_interp_relu_kernel(tc, tab_words, tab_scales, w_words, w_scales, x, wx_words, wx_scales, iw0, iw1, offs, out):
    nc = tc.nc
    with ExitStack() as ctx:
        keep = ctx.enter_context(tc.tile_pool(name="keep", bufs=1))
        prod = ctx.enter_context(tc.psum_pool(name="prod", bufs=4))
        pair = ctx.enter_context(tc.psum_pool(name="pair", bufs=2))
        turn = ctx.enter_context(tc.psum_pool(name="turn", bufs=1))

        offsets = keep.tile([P, 2 * J // 16], U16, name="offsets")
        nc.sync.dma_start(offsets[:], offs)

        table_rows = keep.tile([P, T], U8, name="table_rows", align_bytes=64)
        nc.sync.dma_start(out=table_rows[ROW0:P, :].bitcast(I32), in_=tab_scales[0].bitcast(I32))
        x_raw = keep.tile([P, PACK, J], F32, name="x_raw")
        nc.sync.dma_start(out=x_raw[:], in_=x.rearrange("(p t) j -> p t j", t=PACK))
        wx_plane = keep.tile([P, N], U8, name="wx_plane", align_bytes=64)
        nc.vector.memset(wx_plane[:].bitcast(I32), 0)
        for q in range(4):
            nc.sync.dma_start(out=wx_plane[32 * q : 32 * q + 4, :].bitcast(I32), in_=wx_scales[0, 4 * q : 4 * q + 4, :].bitcast(I32))
        wx_codes = keep.tile([P, 2 * N], U8, name="wx_codes", align_bytes=64)
        nc.sync.dma_start(out=wx_codes[:].bitcast(I32), in_=wx_words[0].bitcast(I32))
        staged = keep.tile([P, PLANE], U8, name="staged", align_bytes=64)
        nc.sync.dma_start(out=staged[ROW0:P, W_COL : W_COL + N].bitcast(I32), in_=w_scales[0].bitcast(I32))
        table = keep.tile([P, T], I32, name="table", align_bytes=64)
        nc.sync.dma_start(out=table[:], in_=tab_words[0].rearrange("p t i -> p (t i)").bitcast(I32))
        iw_rows = keep.tile([P, P], F32, name="iw_rows")
        nc.sync.dma_start(out=iw_rows[IW_ROW : IW_ROW + TILES, :], in_=iw0.rearrange("(a b) -> a b", b=P))
        nc.sync.dma_start(out=iw_rows[IW_ROW + TILES : P, :], in_=iw1.rearrange("(a b) -> a b", b=P))
        w_codes = keep.tile([P, N], I32, name="w_codes", align_bytes=64)
        nc.sync.dma_start(out=w_codes[:], in_=w_words[0].rearrange("p n i -> p (n i)").bitcast(I32))

        nc.vector.memset(table_rows[0:ROW0, :].bitcast(I32), 0)
        planes = keep.tile([P, PLANE], U8, name="planes", align_bytes=64)
        nc.gpsimd.memset(planes[:].bitcast(I32), 0)
        nc.gpsimd.memset(iw_rows[0:IW_ROW, :], 0.0)

        identity = keep.tile([P, P], F32, name="identity")
        ones = keep.tile([P, 32], F32, name="ones")
        ramp = keep.tile([P, 32], F32, name="ramp", align_bytes=64)
        row_id = keep.tile([P, 32], F32, name="row_id", align_bytes=64)
        nc.gpsimd.memset(ones[:], 1.0)
        nc.gpsimd.memset(identity[:], 0.0)
        nc.vector.tensor_tensor_scan(ramp[:], ones[:], ones[:], 0.0, ALU.mult, ALU.add)
        nc.vector.transpose(row_id[:], ramp[:])
        for q in range(4):
            rows = slice(32 * q, 32 * q + 32)
            nc.vector.tensor_tensor(identity[rows, rows], ramp[rows, :], row_id[rows, :], ALU.is_equal)

        picked_rows = keep.tile([P, 2 * J], U8, name="picked_rows", align_bytes=64)
        nc.vector.tensor_copy(picked_rows[:], table_rows[:].indirect(offsets[:]))
        nc.vector.tensor_copy(staged[:, 0 : 2 * J].bitcast(I32), picked_rows[:].bitcast(I32))
        for q in range(4):
            nc.scalar.dma_start(out=planes[32 * q : 32 * q + 4, :].bitcast(I32), in_=staged[ROW0 + 4 * q : ROW0 + 4 * q + 4, :].bitcast(I32))
        w_plane = planes[:, W_COL : W_COL + N]
        picked_plane = [planes[:, g * J : (g + 1) * J] for g in range(2)]


        x_codes = keep.tile([P, J], U32, name="x_codes", align_bytes=64)
        x_plane = keep.tile([P, J], U8, name="x_plane", align_bytes=64)
        x_bf = [keep.tile([P, P, PACK], BF16, name="x_bf%d" % jt, align_bytes=64) for jt in range(TILES)]
        for jt in range(TILES):
            src = x_raw[:, :, jt * P : (jt + 1) * P].rearrange("p t (c i) -> p c t i", i=4)
            dst = x_bf[jt][:].rearrange("p (c i) t -> p c t i", i=4)
            nc.scalar.copy(out=dst, in_=src)
        for jt in range(TILES):
            cols = slice(jt * P, (jt + 1) * P)
            nc.vector.quantize_mx(out=x_codes[:, cols].bitcast(FP8X4), scales=x_plane[:, cols], in_=x_bf[jt][:].rearrange("p j t -> p (j t)"))

        lists = [offsets[:, g * (J // 16) : (g + 1) * (J // 16)] for g in range(2)]

        def turn_into(bank, part, blocks, opens, closes):
            for nt in blocks:
                at = (nt - blocks[0]) * P
                nc.tensor.matmul(
                    bank[:, at : at + P], part[:, nt * P : (nt + 1) * P], identity[:], is_transpose=True,
                    start=(opens and nt == blocks[0]), stop=(closes and nt == blocks[-1]),
                )

        last = TILES - 1
        all_blocks = list(range(TILES))
        sums = [turn.tile([P, N], F32, name="sum%d" % jt) for jt in range(EARLY)]
        skip = [keep.tile([P, N], F32, name="skip%d" % jt) for jt in range(TILES)]

        def project_skip(jt):
            cols = slice(jt * P, (jt + 1) * P)
            bank = pair.tile([P, N], F32, name="pair_bank", tag="pair_bank")
            nc.tensor.matmul_mx(
                out=bank[:], lhsT=x_codes[:, cols].bitcast(FP8X4), lhsT_scale=x_plane[:, cols],
                rhs=wx_codes[:].bitcast(FP4X4), rhs_scale=wx_plane[:], start=True, stop=True,
            )
            if jt < EARLY:
                nc.vector.tensor_copy(out=skip[jt][:], in_=bank[:])
            else:
                nc.scalar.copy(out=skip[jt][:], in_=bank[:])

        for jt in range(EARLY):
            project_skip(jt)
        for jt in range(EARLY):
            turn_into(sums[jt], skip[jt], all_blocks, True, False)
        for jt in range(EARLY, TILES):
            project_skip(jt)

        iw_turned = prod.tile([P, N], F32, name="bank", tag="bank")
        nc.tensor.transpose(iw_turned[:, 0:P], iw_rows[:], identity[:])
        iw_cols = keep.tile([P, 2 * TILES], F32, name="iw_cols")
        nc.scalar.activation(iw_cols[:], iw_turned[:, IW_ROW:P], ACT.Copy)

        picked = [keep.tile([P, J], U32, name="picked%d" % g, align_bytes=64) for g in range(2)]
        for g in range(2):
            nc.vector.tensor_copy(picked[g][:], table[:].bitcast(U32).indirect(lists[g]))

        def project(g, jt):
            cols = slice(jt * P, (jt + 1) * P)
            if g == 1 and jt < 2:
                bank = pair.tile([P, N], F32, name="pair_bank", tag="pair_bank")
            else:
                bank = prod.tile([P, N], F32, name="bank", tag="bank")
            nc.tensor.matmul_mx(
                out=bank[:], lhsT=picked[g][:, cols].bitcast(FP8X4), lhsT_scale=picked_plane[g][:, cols],
                rhs=w_codes[:].bitcast(FP8X4), rhs_scale=w_plane, start=True, stop=True,
            )
            return bank

        first = [keep.tile([P, N], F32, name="first%d" % jt) for jt in range(TILES)]
        for jt in [0, last] + list(range(1, last)):
            bank = project(0, jt)
            if jt < last:
                nc.scalar.activation(first[jt][:], bank[:], ACT.Copy, scale=iw_cols[:, jt : jt + 1])
            else:
                nc.vector.scalar_tensor_tensor(
                    out=first[jt][:], in0=bank[:], scalar=iw_cols[:, jt : jt + 1], in1=skip[jt][:],
                    op0=ALU.mult, op1=ALU.add,
                )

        out_view = out.rearrange("(nt p) j -> p nt j", p=P)
        both = [keep.tile([P, N], F32, name="both%d" % jt) for jt in range(TILES)]
        result = [keep.tile([P, N], F32, name="result%d" % jt) for jt in range(TILES)]

        halves = [all_blocks[:2], all_blocks[2:]]
        for jt in range(TILES):
            bank = project(1, jt)
            for blocks in ([all_blocks] if jt < last else halves):
                cols = slice(blocks[0] * P, (blocks[-1] + 1) * P)
                nc.vector.scalar_tensor_tensor(
                    out=both[jt][:, cols], in0=bank[:, cols], scalar=iw_cols[:, TILES + jt : TILES + jt + 1],
                    in1=first[jt][:, cols], op0=ALU.mult, op1=ALU.add,
                )

        for jt in range(TILES):
            pieces = [all_blocks] if jt < last else halves
            for blocks in pieces:
                if jt < EARLY:
                    bank = sums[jt]
                elif blocks[0] == 0:
                    bank = prod.tile([P, N], F32, name="bank", tag="bank")
                else:
                    bank = pair.tile([P, N], F32, name="pair_bank", tag="pair_bank")
                if EARLY <= jt < last:
                    turn_into(bank, skip[jt], blocks, True, False)
                cols = slice(blocks[0] * P, (blocks[-1] + 1) * P)
                width = len(blocks) * P
                turn_into(bank, both[jt], blocks, jt == last, True)
                if jt < last:
                    nc.scalar.activation(result[jt][:, cols], bank[:, 0:width], ACT.Relu)
                else:
                    nc.vector.tensor_scalar_max(result[jt][:, cols], bank[:, 0:width], 0.0)
                nc.sync.dma_start(
                    out=out_view[:, blocks[0] : blocks[-1] + 1, jt * P : (jt + 1) * P],
                    in_=result[jt][:, cols].rearrange("p (nt j) -> p nt j", j=P),
                )
